import numpy as np
import ml_dtypes


def mxq(x, axis, fmt="e4m3"):
    dtype, down = {"e4m3": (ml_dtypes.float8_e4m3fn, 7), "e5m2": (ml_dtypes.float8_e5m2, 14)}[fmt]
    v = np.moveaxis(np.asarray(x, np.float32).astype(ml_dtypes.bfloat16).astype(np.float64), axis, -1)
    blocks = v.reshape(v.shape[:-1] + (-1, 32))
    amax = np.abs(blocks).max(-1, keepdims=True)
    byte = np.maximum(np.where(amax > 0, np.frexp(amax)[1] - 1 + 127, 0) - down, 1)
    scale = np.exp2(byte - 127.0)
    codes = (blocks / scale).astype(np.float32).astype(dtype).astype(np.float64)
    return np.moveaxis((codes * scale).reshape(v.shape), -1, axis)


WIDE = False


def mx_kscale(k):
    if not WIDE:
        return np.ones(k)
    levels = np.array([10, -10, 5, -5, 0])
    if k % 512:
        return np.exp2(np.random.permutation(np.resize(levels, k // 32))).repeat(32)
    a = np.empty((k // 512, 16))
    for p in range(k // 512):
        a[p, :8] = np.random.permutation(np.resize(levels, 8))
        for g in range(8):
            far = levels[np.abs(levels - a[p, g]) >= 10]
            a[p, g + 8] = far[np.random.randint(len(far))]
    return np.exp2(a.ravel()).repeat(32)


def f64(x):
    return np.asarray(x).astype(np.float64)


def striped(idx):
    return np.tile(idx.reshape(-1, 16).T, (8, 1)).astype(np.uint16)


def unstriped(offs):
    return offs[:16].T.reshape(-1).astype(np.int64)


E2M1 = np.array([0.0, 0.5, 1.0, 1.5, 2.0, 3.0, 4.0, 6.0, -0.0, -0.5, -1.0, -1.5, -2.0, -3.0, -4.0, -6.0])


def pack_weight(w, fmt):
    k, n = w.shape
    w = f64(np.asarray(w, np.float32).astype(ml_dtypes.bfloat16)).reshape(k // 32, 32, n)
    amax = np.abs(w).max(1)
    if fmt == "e4m3":
        byte = np.frexp(amax)[1] - 1 + 127 - 7
    else:
        mant, ex = np.frexp(amax / 6.0)
        byte = np.where(mant > 0.5, ex, ex - 1) + 127
    byte = np.clip(np.where(amax > 0, byte, 1), 1, 254)
    scaled = (w * np.exp2(127.0 - byte)[:, None, :]).reshape(k, n).astype(np.float32)
    by_word = np.ascontiguousarray(scaled.reshape(k // 512, 128, 4, n).transpose(0, 1, 3, 2))
    if fmt == "e4m3":
        words = by_word.astype(ml_dtypes.float8_e4m3fn).view(np.uint8)
    else:
        c = by_word.astype(ml_dtypes.float4_e2m1fn).view(np.uint8) & 0xF
        words = (c[..., 0::2] | (c[..., 1::2] << 4)).reshape(k // 512, 128, 2 * n)
    return np.ascontiguousarray(words), np.ascontiguousarray(byte.astype(np.uint8).reshape(k // 512, 16, n))


def unpack_weight(words, scales, fmt):
    g, _, n = scales.shape
    words = np.ascontiguousarray(words).reshape(g, 128, n, -1)
    if fmt == "e4m3":
        vals = words.view(ml_dtypes.float8_e4m3fn).astype(np.float64)
    else:
        nib = np.empty((g, 128, n, 4), np.uint8)
        nib[..., 0::2] = words & 0xF
        nib[..., 1::2] = words >> 4
        vals = E2M1[nib]
    vals = vals * np.repeat(np.exp2(scales.astype(np.float64) - 127.0), 8, axis=1)[..., None]
    return vals.transpose(0, 1, 3, 2).reshape(g * 512, n)


def gelu(v):
    return 0.5 * v * (1.0 + np.tanh(np.sqrt(2.0 / np.pi) * (v + 0.044715 * v**3)))


def striped8(idx):
    return np.concatenate([v.reshape(-1, 16).T for v in idx]).astype(np.uint16)


def unstriped8(offs):
    return np.stack([offs[16 * g:16 * g + 16].T.reshape(-1) for g in range(8)]).astype(np.int64)


def heads(xT, wgt, idx8):
    k = np.arange(xT.shape[0])
    return wgt[k // 4 % 128] * xT[k[:, None], idx8[k % 512 // 64]]


K, T, S, R, N, G, P = 1024, 2048, 1024, 1024, 512, 8, 16

def setup_inputs():
    n = np.random.standard_normal
    s = mx_kscale(K)[:, None]
    u = mx_kscale(R)[:, None]
    xT = (n((K, T)) * s).astype(np.float32)
    wgt = np.repeat(np.random.uniform(0.5, 2.0, (G, S)), P, axis=0).astype(np.float32)
    offs = striped8(np.stack([np.random.permutation(T)[:S] for _ in range(G)]))
    w1 = (n((K, R)) / np.sqrt(K) / s).astype(np.float32)
    c = (np.random.uniform(0.5, 2.0, R) * u[:, 0]).astype(np.float32)
    kg_words, kg_scales = pack_weight(n((R, N)) / np.sqrt(R) / u, "e2m1")
    return {"xT": xT, "wgt": wgt, "offs": offs, "w1": w1, "c": c,
            "kg_words": kg_words, "kg_scales": kg_scales}

def reference(xT, wgt, offs, w1, c, kg_words, kg_scales):
    xg = mxq(heads(f64(xT), f64(wgt), unstriped8(offs)), 0, "e4m3")
    w1q = mxq(f64(w1), 0, "e4m3")
    res = w1q.T @ xg
    h = f64(c)[:, None] * (res * np.reciprocal(1.0 + np.square(res)))
    hq = mxq(h, 0, "e4m3")
    kg = unpack_weight(kg_words, kg_scales, "e2m1")
    return kg.T @ hq

@@ -1,0 +1,248 @@
+from contextlib import ExitStack
+
+import concourse.mybir as mybir
+
+K, T, S, R, N = 1024, 2048, 1024, 1024, 512
+FLOPS = 2 * K * R * S + 2 * R * N * S
+
+F32 = mybir.dt.float32
+BF16 = mybir.dt.bfloat16
+I32 = mybir.dt.int32
+U32 = mybir.dt.uint32
+U16 = mybir.dt.uint16
+U8 = mybir.dt.uint8
+FP8X4 = mybir.dt.float8_e4m3fn_x4
+FP4X4 = mybir.dt.float4_e2m1fn_x4
+MULT = mybir.AluOpType.mult
+ACT = mybir.ActivationFunctionType
+
+P = 128
+PACK = 4
+PASS = P * PACK
+JC = 512
+
+
+def tile_list_delayed_residual_correction_kernel(tc, xT, wgt, offs, w1, c, kg_words, kg_scales, out):
+    nc = tc.nc
+    with ExitStack() as ctx:
+        keep = ctx.enter_context(tc.tile_pool(name="keep", bufs=1))
+        ring = ctx.enter_context(tc.tile_pool(name="ring", bufs=2))
+        psum = ctx.enter_context(tc.psum_pool(name="psum", bufs=8))
+
+        offsets = keep.tile([P, S // 16], U16, name="offsets")
+        nc.sync.dma_start(offsets[:], offs)
+
+        warm = keep.tile([P, 8], F32, name="warm")
+        warm2 = keep.tile([P, 8], F32, name="warm2")
+        nc.vector.memset(warm[:], 1.0)
+        nc.scalar.activation(out=warm2[:], in_=warm[:], func=ACT.Abs_reciprocal_sqrt, bias=1.0)
+
+        kg_plane = keep.tile([P, 2, N], U8, name="kg_plane", align_bytes=64)
+        nc.vector.memset(kg_plane[:].rearrange("p a n -> p (a n)").bitcast(I32), 0)
+
+        x_src = xT.rearrange("(a p i) t -> a i p t", a=2, i=PACK)
+        w_src = w1.rearrange("(a p i) (b r) -> a b p i r", a=2, i=PACK, b=2)
+        trust = [keep.tile([P, JC], F32, name="trust%d" % h) for h in range(2)]
+        planes = {}
+        w_raw = {}
+
+        def load_trust(h):
+            nc.sync.dma_start(trust[h][:], wgt[:, h * JC : (h + 1) * JC])
+
+        def load_plane(a, i):
+            planes[a, i] = keep.tile([P, T], F32, name="plane%d%d" % (a, i))
+            nc.sync.dma_start(planes[a, i][:], x_src[a, i])
+
+        def load_w(a, b):
+            w_raw[a, b] = keep.tile([P, PACK, PASS], F32, name="w_raw%d%d" % (a, b))
+            nc.sync.dma_start(w_raw[a, b][:], w_src[a, b])
+
+        gain = keep.tile([P, 2, PACK], F32, name="gain")
+        kg_codes = keep.tile([P, 2, 2 * N], U8, name="kg_codes", align_bytes=64)
+
+        load_trust(0)
+        load_plane(0, 0)
+        load_trust(1)
+        load_plane(0, 1)
+        load_plane(0, 2)
+        load_plane(0, 3)
+        load_plane(1, 0)
+        load_w(0, 0)
+        load_plane(1, 1)
+        load_w(1, 0)
+        load_plane(1, 2)
+        load_plane(1, 3)
+        nc.sync.dma_start(gain[:], c.rearrange("(b p t) -> p b t", b=2, t=PACK))
+        load_w(0, 1)
+        load_w(1, 1)
+        nc.sync.dma_start(kg_codes[:].bitcast(I32), kg_words.bitcast(I32).rearrange("a p w -> p a w"))
+        for q in range(4):
+            nc.sync.dma_start(
+                kg_plane[32 * q : 32 * q + 4, :, :].bitcast(I32),
+                kg_scales.bitcast(I32)[:, 4 * q : 4 * q + 4, :].rearrange("a r w -> r a w"),
+            )
+
+        def quantize(name, woven, width):
+            codes = keep.tile([P, width], U32, name=name + "_codes", align_bytes=64)
+            scales = keep.tile([P, width], U8, name=name + "_scales", align_bytes=64)
+            nc.vector.quantize_mx(out=codes[:].bitcast(FP8X4), scales=scales[:], in_=woven[:])
+            return codes, scales
+
+        def copy_on(engine, dst, src):
+            if engine == "scalar":
+                nc.scalar.copy(out=dst, in_=src)
+            else:
+                nc.vector.tensor_copy(out=dst, in_=src)
+
+        w_woven, wq, picked, x_woven, xq, hq, h_woven = {}, {}, {}, {}, {}, {}, {}
+
+        shared = keep.tile([P, 2 * PACK - 2, JC], F32, name="shared")
+        picked[1, 1] = shared[:, 0:PACK, :]
+        picked[1, 0] = shared[:, PACK - 2 :, :]
+
+        spare = keep.tile([P, 2, JC], F32, name="spare", align_bytes=64)
+
+        for b in range(2):
+            for h in range(2):
+                hq[b, h] = (
+                    keep.tile([P, JC], U32, name="hq%d%d_codes" % (b, h), align_bytes=64),
+                    keep.tile([P, JC], U8, name="hq%d%d_scales" % (b, h), align_bytes=64),
+                )
+
+        def weave_w(a, b, engine):
+            w_woven[a, b] = ring.tile([P, PACK * PASS], BF16, name="w_woven", align_bytes=64)
+            copy_on(
+                engine,
+                w_woven[a, b][:].rearrange("p (t m i) -> p m i t", t=PACK, i=PACK),
+                w_raw[a, b][:].rearrange("p i (m t) -> p m i t", t=PACK),
+            )
+
+        def quant_w(a, b):
+            wq[a, b] = quantize("wq%d%d" % (a, b), w_woven[a, b], PASS)
+
+        def gather(a, i, h):
+            if a == 0 and i == 0:
+                picked[a, h] = ring.tile([P, PACK, JC], F32, name="picked")
+            cols = slice(h * JC // 16, (h + 1) * JC // 16)
+            nc.vector.tensor_tensor(picked[a, h][:, i, :], planes[a, i][:].indirect(offsets[:, cols]), trust[h][:], MULT)
+
+        def weave_x(a, h, engine, held=None):
+            if held is None:
+                x_woven[a, h] = ring.tile([P, PACK * JC], BF16, name="x_woven", align_bytes=64)
+            else:
+                x_woven[a, h] = held[:].rearrange("p g n -> p (g n)").bitcast(BF16)
+            copy_on(
+                engine,
+                x_woven[a, h][:].rearrange("p (m e i) -> p m i e", e=4, i=PACK),
+                picked[a, h].rearrange("p i (m e) -> p m i e", e=4),
+            )
+
+        def quant_x(a, h):
+            xq[a, h] = quantize("xq%d%d" % (a, h), x_woven[a, h], JC)
+
+        def damp(b, j0, width, order=(1, 0), held=None):
+            h, steps = j0 // JC, slice(j0 % JC, j0 % JC + width)
+            per_bank = JC // width
+            root = ring.tile([P, PACK, width], F32, name="root")
+            part = ring.tile([P, PACK, width], F32, name="part")
+            group = per_bank
+            for t0 in range(0, PACK, group):
+                if held is not None and t0 == held[0]:
+                    square = held[1][:, 0:group, :]
+                else:
+                    square = ring.tile([P, group, width], F32, name="square", bufs=3)
+                sums = {}
+                for tb in range(t0, t0 + group, per_bank):
+                    bank = psum.tile([P, per_bank, width], F32, name="bank")
+                    for t in range(tb, tb + per_bank):
+                        sums[t] = bank[:, t - tb, :]
+                        cols = slice(t * P, (t + 1) * P)
+                        for a in order:
+                            nc.tensor.matmul_mx(
+                                out=sums[t],
+                                lhsT=wq[a, b][0][:, cols].bitcast(FP8X4),
+                                lhsT_scale=wq[a, b][1][:, cols],
+                                rhs=xq[a, h][0][:, steps].bitcast(FP8X4),
+                                rhs_scale=xq[a, h][1][:, steps],
+                                start=(a == order[0]),
+                                stop=(a == order[1]),
+                            )
+                    nc.scalar.activation(out=square[:, tb - t0 : tb - t0 + per_bank, :], in_=bank[:], func=ACT.Square)
+                nc.scalar.activation(out=root[:, t0 : t0 + group, :], in_=square[:, :, :], func=ACT.Abs_reciprocal_sqrt, bias=1.0)
+                for t in range(t0, t0 + group):
+                    nc.vector.scalar_tensor_tensor(
+                        out=part[:, t, :], in0=sums[t], scalar=gain[:, b, t : t + 1], in1=root[:, t, :], op0=MULT, op1=MULT
+                    )
+            h_woven[b, j0] = ring.tile([P, PACK * width], BF16, name="h_woven", align_bytes=64)
+            nc.vector.tensor_tensor(
+                h_woven[b, j0][:].rearrange("p (m e t) -> p m t e", e=4, t=PACK),
+                part[:].rearrange("p t (m e) -> p m t e", e=4),
+                root[:].rearrange("p t (m e) -> p m t e", e=4),
+                MULT,
+            )
+            nc.vector.quantize_mx(out=hq[b, h][0][:, steps].bitcast(FP8X4), scales=hq[b, h][1][:, steps], in_=h_woven[b, j0][:])
+
+        def correct(j0, width, engines, order=(1, 0)):
+            piece = JC if width == JC else P
+            per_bank = JC // width
+            for n0 in range(0, N // P, per_bank):
+                bank = psum.tile([P, per_bank, width], F32, name="bank")
+                for nt in range(n0, n0 + per_bank):
+                    for c0 in range(0, width, piece):
+                        for b in order:
+                            nc.tensor.matmul_mx(
+                                out=bank[:, nt - n0, c0 : c0 + piece],
+                                lhsT=kg_codes[:, b, 2 * nt * P : 2 * (nt + 1) * P].bitcast(FP4X4),
+                                lhsT_scale=kg_plane[:, b, nt * P : (nt + 1) * P],
+                                rhs=hq[b, j0 // JC][0][:, j0 % JC + c0 : j0 % JC + c0 + piece].bitcast(FP8X4),
+                                rhs_scale=hq[b, j0 // JC][1][:, j0 % JC + c0 : j0 % JC + c0 + piece],
+                                start=(b == order[0]),
+                                stop=(b == order[1]),
+                            )
+                result = ring.tile([P, per_bank, width], F32, name="result", bufs=4)
+                copy_on(engines[(n0 // per_bank) % len(engines)], result[:], bank[:])
+                rows = out[n0 * P : (n0 + per_bank) * P, j0 : j0 + width]
+                nc.sync.dma_start(rows.rearrange("(g p) j -> p g j", p=P), result[:])
+
+        gather(0, 0, 0)
+        gather(0, 0, 1)
+        gather(0, 1, 0)
+        gather(0, 1, 1)
+        gather(0, 2, 0)
+        gather(0, 2, 1)
+        gather(0, 3, 0)
+        gather(0, 3, 1)
+        weave_x(0, 0, "scalar")
+        weave_x(0, 1, "scalar")
+        gather(1, 0, 0)
+        gather(1, 0, 1)
+        quant_x(0, 0)
+        weave_w(0, 0, "scalar")
+        gather(1, 1, 0)
+        gather(1, 1, 1)
+        quant_x(0, 1)
+        weave_w(1, 0, "scalar")
+        quant_w(0, 0)
+        gather(1, 2, 0)
+        quant_w(1, 0)
+        gather(1, 3, 0)
+        weave_x(1, 0, "vector")
+        quant_x(1, 0)
+        weave_w(0, 1, "scalar")
+        gather(1, 2, 1)
+        gather(1, 3, 1)
+        weave_w(1, 1, "vector")
+        quant_w(0, 1)
+        quant_w(1, 1)
+        damp(0, 0, 512, (0, 1), held=(2, spare))
+        weave_x(1, 1, "scalar", spare)
+        quant_x(1, 1)
+        damp(1, 0, 512)
+        damp(0, 512, 512)
+        damp(1, 512, 256)
+        damp(1, 768, 128)
+        damp(1, 896, 128)
+        correct(0, 512, ["scalar"])
+        correct(512, 256, ["scalar"])
+        correct(768, 128, ["scalar"])
+        correct(896, 128, ["scalar"])

@@ -14,6 +14,7 @@ U8 = mybir.dt.uint8
 FP8X4 = mybir.dt.float8_e4m3fn_x4
 FP4X4 = mybir.dt.float4_e2m1fn_x4
 MULT = mybir.AluOpType.mult
+ADD = mybir.AluOpType.add
 ACT = mybir.ActivationFunctionType
 
 P = 128
@@ -54,7 +55,7 @@ def tile_list_delayed_residual_correction_kernel(tc, xT, wgt, offs, w1, c, kg_wo
             nc.sync.dma_start(planes[a, i][:], x_src[a, i])
 
         def load_w(a, b):
-            w_raw[a, b] = keep.tile([P, PACK, PASS], F32, name="w_raw%d%d" % (a, b))
+            w_raw[a, b] = keep.tile([P, PACK, PASS], F32, name="w_raw%d%d" % (a, b), align_bytes=64)
             nc.sync.dma_start(w_raw[a, b][:], w_src[a, b])
 
         gain = keep.tile([P, 2, PACK], F32, name="gain")
@@ -91,16 +92,15 @@ def tile_list_delayed_residual_correction_kernel(tc, xT, wgt, offs, w1, c, kg_wo
         def copy_on(engine, dst, src):
             if engine == "scalar":
                 nc.scalar.copy(out=dst, in_=src)
+            elif engine == "gpsimd":
+                nc.gpsimd.tensor_scalar(out=dst, in0=src, scalar1=1.0, scalar2=0.0, op0=MULT, op1=ADD)
             else:
                 nc.vector.tensor_copy(out=dst, in_=src)
 
         w_woven, wq, picked, x_woven, xq, hq, h_woven = {}, {}, {}, {}, {}, {}, {}
 
-        shared = keep.tile([P, 2 * PACK - 2, JC], F32, name="shared")
-        picked[1, 1] = shared[:, 0:PACK, :]
-        picked[1, 0] = shared[:, PACK - 2 :, :]
-
-        spare = keep.tile([P, 2, JC], F32, name="spare", align_bytes=64)
+        early = [keep.tile([P, 2, JC], F32, name="early%d" % h) for h in range(2)]
+        late = keep.tile([P, 2, JC], F32, name="late")
 
         for b in range(2):
             for h in range(2):
@@ -111,11 +111,10 @@ def tile_list_delayed_residual_correction_kernel(tc, xT, wgt, offs, w1, c, kg_wo
 
         def weave_w(a, b, engine):
             w_woven[a, b] = ring.tile([P, PACK * PASS], BF16, name="w_woven", align_bytes=64)
-            copy_on(
-                engine,
-                w_woven[a, b][:].rearrange("p (t m i) -> p m i t", t=PACK, i=PACK),
-                w_raw[a, b][:].rearrange("p i (m t) -> p m i t", t=PACK),
-            )
+            dst = w_woven[a, b][:].rearrange("p (u e m i) -> p u m i e", u=2, e=2, i=PACK)
+            src = w_raw[a, b][:].rearrange("p i (m u e) -> p u m i e", u=2, e=2)
+            for u in range(2):
+                copy_on(engine.split("+")[u % len(engine.split("+"))], dst[:, u], src[:, u])
 
         def quant_w(a, b):
             wq[a, b] = quantize("wq%d%d" % (a, b), w_woven[a, b], PASS)
@@ -124,7 +123,17 @@ def tile_list_delayed_residual_correction_kernel(tc, xT, wgt, offs, w1, c, kg_wo
             if a == 0 and i == 0:
                 picked[a, h] = ring.tile([P, PACK, JC], F32, name="picked")
             cols = slice(h * JC // 16, (h + 1) * JC // 16)
-            nc.vector.tensor_tensor(picked[a, h][:, i, :], planes[a, i][:].indirect(offsets[:, cols]), trust[h][:], MULT)
+            dst = picked[a, h][:, i, :] if a == 0 else (early[h], late)[i // 2][:, i % 2, :]
+            nc.vector.tensor_tensor(dst, planes[a, i][:].indirect(offsets[:, cols]), trust[h][:], MULT)
+
+        def weave_pair(a, h, u, engine):
+            if u == 0:
+                x_woven[a, h] = w_raw[1, 0][:, 2 * h : 2 * h + 2, :].rearrange("p g n -> p (g n)").bitcast(BF16)
+            copy_on(
+                engine,
+                x_woven[a, h][:].rearrange("p (n i) -> p n i", i=PACK)[:, :, 2 * u : 2 * u + 2],
+                (early[h], late)[u][:].rearrange("p i n -> p n i"),
+            )
 
         def weave_x(a, h, engine, held=None):
             if held is None:
@@ -133,18 +142,18 @@ def tile_list_delayed_residual_correction_kernel(tc, xT, wgt, offs, w1, c, kg_wo
                 x_woven[a, h] = held[:].rearrange("p g n -> p (g n)").bitcast(BF16)
             copy_on(
                 engine,
-                x_woven[a, h][:].rearrange("p (m e i) -> p m i e", e=4, i=PACK),
-                picked[a, h].rearrange("p i (m e) -> p m i e", e=4),
+                x_woven[a, h][:].rearrange("p (m e i) -> p m i e", e=2, i=PACK),
+                picked[a, h].rearrange("p i (m e) -> p m i e", e=2),
             )
 
         def quant_x(a, h):
             xq[a, h] = quantize("xq%d%d" % (a, h), x_woven[a, h], JC)
 
-        def damp(b, j0, width, order=(1, 0), held=None):
+        def damp(b, j0, width, order=(1, 0), held=None, on_scalar=(), share=0):
             h, steps = j0 // JC, slice(j0 % JC, j0 % JC + width)
             per_bank = JC // width
-            root = ring.tile([P, PACK, width], F32, name="root")
-            part = ring.tile([P, PACK, width], F32, name="part")
+            root = ring.tile([P, PACK, width], F32, name="root", bufs=2)
+            part = ring.tile([P, PACK, width], F32, name="part", bufs=2)
             group = per_bank
             for t0 in range(0, PACK, group):
                 if held is not None and t0 == held[0]:
@@ -168,18 +177,35 @@ def tile_list_delayed_residual_correction_kernel(tc, xT, wgt, offs, w1, c, kg_wo
                                 stop=(a == order[1]),
                             )
                     nc.scalar.activation(out=square[:, tb - t0 : tb - t0 + per_bank, :], in_=bank[:], func=ACT.Square)
-                nc.scalar.activation(out=root[:, t0 : t0 + group, :], in_=square[:, :, :], func=ACT.Abs_reciprocal_sqrt, bias=1.0)
+                if t0 in on_scalar:
+                    half = ring.tile([P, group, width], F32, name="half")
+                    nc.scalar.activation(out=half[:], in_=square[:, :, :], func=ACT.Abs_reciprocal_sqrt, bias=1.0)
+                    nc.scalar.activation(out=root[:, t0 : t0 + group, :], in_=half[:], func=ACT.Square)
+                else:
+                    nc.scalar.activation(out=root[:, t0 : t0 + group, :], in_=square[:, :, :], func=ACT.Abs_reciprocal_sqrt, bias=1.0)
                 for t in range(t0, t0 + group):
-                    nc.vector.scalar_tensor_tensor(
-                        out=part[:, t, :], in0=sums[t], scalar=gain[:, b, t : t + 1], in1=root[:, t, :], op0=MULT, op1=MULT
-                    )
+                    if t in on_scalar:
+                        nc.scalar.activation(out=part[:, t, :], in_=sums[t], func=ACT.Copy, scale=gain[:, b, t : t + 1])
+                    else:
+                        nc.vector.scalar_tensor_tensor(
+                            out=part[:, t, :], in0=sums[t], scalar=gain[:, b, t : t + 1], in1=root[:, t, :], op0=MULT, op1=MULT
+                        )
             h_woven[b, j0] = ring.tile([P, PACK * width], BF16, name="h_woven", align_bytes=64)
-            nc.vector.tensor_tensor(
-                h_woven[b, j0][:].rearrange("p (m e t) -> p m t e", e=4, t=PACK),
-                part[:].rearrange("p t (m e) -> p m t e", e=4),
-                root[:].rearrange("p t (m e) -> p m t e", e=4),
-                MULT,
-            )
+            lo = max(share - 4, 0)
+            if share < width:
+                nc.vector.tensor_tensor(
+                    h_woven[b, j0][:, PACK * lo :].rearrange("p (m e t) -> p m t e", e=2, t=PACK),
+                    part[:, :, lo:].rearrange("p t (m e) -> p m t e", e=2),
+                    root[:, :, lo:].rearrange("p t (m e) -> p m t e", e=2),
+                    MULT,
+                )
+            if share:
+                nc.gpsimd.tensor_tensor(
+                    h_woven[b, j0][:, 0 : PACK * share].rearrange("p (n t) -> p n t", t=PACK),
+                    part[:, :, 0:share].rearrange("p t n -> p n t"),
+                    root[:, :, 0:share].rearrange("p t n -> p n t"),
+                    MULT,
+                )
             nc.vector.quantize_mx(out=hq[b, h][0][:, steps].bitcast(FP8X4), scales=hq[b, h][1][:, steps], in_=h_woven[b, j0][:])
 
         def correct(j0, width, engines, order=(1, 0)):
@@ -204,6 +230,24 @@ def tile_list_delayed_residual_correction_kernel(tc, xT, wgt, offs, w1, c, kg_wo
                 rows = out[n0 * P : (n0 + per_bank) * P, j0 : j0 + width]
                 nc.sync.dma_start(rows.rearrange("(g p) j -> p g j", p=P), result[:])
 
+        def correct_last(j0, width):
+            h, steps = j0 // JC, slice(j0 % JC, j0 % JC + width)
+            result = ring.tile([P, N // P, width], F32, name="result", bufs=4)
+            for nt in range(N // P):
+                bank = psum.tile([P, width], F32, name="bank")
+                for b in range(2):
+                    nc.tensor.matmul_mx(
+                        out=bank[:],
+                        lhsT=kg_codes[:, b, 2 * nt * P : 2 * (nt + 1) * P].bitcast(FP4X4),
+                        lhsT_scale=kg_plane[:, b, nt * P : (nt + 1) * P],
+                        rhs=hq[b, h][0][:, steps].bitcast(FP8X4),
+                        rhs_scale=hq[b, h][1][:, steps],
+                        start=(b == 0),
+                        stop=(b == 1),
+                    )
+                copy_on(("scalar", "vector")[nt % 2], result[:, nt, :], bank[:])
+            nc.sync.dma_start(out[:, j0 : j0 + width].rearrange("(g p) j -> p g j", p=P), result[:])
+
         gather(0, 0, 0)
         gather(0, 0, 1)
         gather(0, 1, 0)
@@ -223,10 +267,12 @@ def tile_list_delayed_residual_correction_kernel(tc, xT, wgt, offs, w1, c, kg_wo
         quant_x(0, 1)
         weave_w(1, 0, "scalar")
         quant_w(0, 0)
+        weave_pair(1, 0, 0, "scalar")
+        weave_pair(1, 1, 0, "scalar")
         gather(1, 2, 0)
         quant_w(1, 0)
         gather(1, 3, 0)
-        weave_x(1, 0, "vector")
+        weave_pair(1, 0, 1, "vector")
         quant_x(1, 0)
         weave_w(0, 1, "scalar")
         gather(1, 2, 1)
@@ -234,15 +280,15 @@ def tile_list_delayed_residual_correction_kernel(tc, xT, wgt, offs, w1, c, kg_wo
         weave_w(1, 1, "vector")
         quant_w(0, 1)
         quant_w(1, 1)
-        damp(0, 0, 512, (0, 1), held=(2, spare))
-        weave_x(1, 1, "scalar", spare)
+        damp(0, 0, 512, (0, 1))
+        weave_pair(1, 1, 1, "scalar")
         quant_x(1, 1)
-        damp(1, 0, 512)
-        damp(0, 512, 512)
-        damp(1, 512, 256)
-        damp(1, 768, 128)
+        damp(1, 0, 512, on_scalar=(3,))
+        damp(0, 512, 512, on_scalar=(3,))
+        damp(1, 512, 256, on_scalar=())
+        damp(1, 768, 128, on_scalar=())
         damp(1, 896, 128)
         correct(0, 512, ["scalar"])
         correct(512, 256, ["scalar"])
         correct(768, 128, ["scalar"])
-        correct(896, 128, ["scalar"])
+        correct_last(896, 128)

@@ -14,13 +14,18 @@ U8 = mybir.dt.uint8
 FP8X4 = mybir.dt.float8_e4m3fn_x4
 FP4X4 = mybir.dt.float4_e2m1fn_x4
 MULT = mybir.AluOpType.mult
-ADD = mybir.AluOpType.add
 ACT = mybir.ActivationFunctionType
 
 P = 128
 PACK = 4
 PASS = P * PACK
-JC = 512
+HALF = S // 2
+LIST_ROWS = 16
+RUN = 4
+QUARTER = S // 4
+BLOCK = 32
+HELD = 2
+TAIL = (256, 128, 128)
 
 
 def tile_list_delayed_residual_correction_kernel(tc, xT, wgt, offs, w1, c, kg_words, kg_scales, out):
@@ -30,52 +35,55 @@ def tile_list_delayed_residual_correction_kernel(tc, xT, wgt, offs, w1, c, kg_wo
         ring = ctx.enter_context(tc.tile_pool(name="ring", bufs=2))
         psum = ctx.enter_context(tc.psum_pool(name="psum", bufs=8))
 
-        offsets = keep.tile([P, S // 16], U16, name="offsets")
-        nc.sync.dma_start(offsets[:], offs)
+        offsets = keep.tile([P, S // LIST_ROWS], U16, name="offsets")
 
-        warm = keep.tile([P, 8], F32, name="warm")
-        warm2 = keep.tile([P, 8], F32, name="warm2")
-        nc.vector.memset(warm[:], 1.0)
-        nc.scalar.activation(out=warm2[:], in_=warm[:], func=ACT.Abs_reciprocal_sqrt, bias=1.0)
+        warm_in = keep.tile([P, 8], F32, name="warm_in")
+        warm_out = keep.tile([P, 8], F32, name="warm_out")
+        nc.vector.memset(warm_in[:], 1.0)
+        nc.scalar.activation(out=warm_out[:], in_=warm_in[:], func=ACT.Abs_reciprocal_sqrt, bias=1.0)
 
         kg_plane = keep.tile([P, 2, N], U8, name="kg_plane", align_bytes=64)
         nc.vector.memset(kg_plane[:].rearrange("p a n -> p (a n)").bitcast(I32), 0)
 
-        x_src = xT.rearrange("(a p i) t -> a i p t", a=2, i=PACK)
-        w_src = w1.rearrange("(a p i) (b r) -> a b p i r", a=2, i=PACK, b=2)
-        trust = [keep.tile([P, JC], F32, name="trust%d" % h) for h in range(2)]
-        planes = {}
-        w_raw = {}
+        trust_part = keep.tile([P, QUARTER], F32, name="trust_part", align_bytes=64)
+        for q in range(4):
+            nc.sync.dma_start(trust_part[q:P:4, :], wgt[q:P:4, q * QUARTER : (q + 1) * QUARTER])
+        nc.sync.dma_start(offsets[:], offs)
+        trust_turned = keep.tile([P, QUARTER], F32, name="trust_turned", align_bytes=64)
+        nc.vector.transpose(trust_turned[:], trust_part[:])
+        trust_spread = ring.tile([P, S], F32, name="scaled", align_bytes=64)
+        by_row = trust_turned[:].rearrange("p (c r q) -> p q c r", r=BLOCK // 4, q=4)
+        for h in range(2):
+            nc.vector.tensor_copy(
+                out=trust_spread[:, h * HALF : (h + 1) * HALF].rearrange("p (q c r e) -> p q c r e", q=2, r=BLOCK // 4, e=4),
+                in_=by_row[:, 2 * h : 2 * h + 2].unsqueeze(4).to_broadcast([P, 2, QUARTER // BLOCK, BLOCK // 4, 4]),
+            )
+        trust = [keep.tile([P, HALF], F32, name="trust%d" % h, align_bytes=64) for h in range(2)]
+        for h in range(2):
+            nc.vector.transpose(trust[h][:], trust_spread[:, h * HALF : (h + 1) * HALF])
 
-        def load_trust(h):
-            nc.sync.dma_start(trust[h][:], wgt[:, h * JC : (h + 1) * JC])
+        x_rows = xT.rearrange("(a p i) t -> a i p t", a=2, i=PACK)
+        w_rows = w1.rearrange("(a p i) (b r) -> a b p i r", a=2, i=PACK, b=2)
+        planes, w_raw = {}, {}
 
         def load_plane(a, i):
             planes[a, i] = keep.tile([P, T], F32, name="plane%d%d" % (a, i))
-            nc.sync.dma_start(planes[a, i][:], x_src[a, i])
+            nc.sync.dma_start(planes[a, i][:], x_rows[a, i])
 
         def load_w(a, b):
-            w_raw[a, b] = keep.tile([P, PACK, PASS], F32, name="w_raw%d%d" % (a, b), align_bytes=64)
-            nc.sync.dma_start(w_raw[a, b][:], w_src[a, b])
+            w_raw[a, b] = keep.tile([P, PACK, PASS], F32, name="w_raw%d%d" % (a, b))
+            nc.sync.dma_start(w_raw[a, b][:], w_rows[a, b])
 
-        gain = keep.tile([P, 2, PACK], F32, name="gain")
-        kg_codes = keep.tile([P, 2, 2 * N], U8, name="kg_codes", align_bytes=64)
-
-        load_trust(0)
-        load_plane(0, 0)
-        load_trust(1)
-        load_plane(0, 1)
-        load_plane(0, 2)
-        load_plane(0, 3)
-        load_plane(1, 0)
+        for n in range(2 * PACK - 1):
+            load_plane(n // PACK, n % PACK)
         load_w(0, 0)
-        load_plane(1, 1)
+        load_plane(1, PACK - 1)
         load_w(1, 0)
-        load_plane(1, 2)
-        load_plane(1, 3)
-        nc.sync.dma_start(gain[:], c.rearrange("(b p t) -> p b t", b=2, t=PACK))
         load_w(0, 1)
         load_w(1, 1)
+        gain = keep.tile([P, 2, PACK], F32, name="gain")
+        nc.sync.dma_start(gain[:], c.rearrange("(b p t) -> p b t", b=2, t=PACK))
+        kg_codes = keep.tile([P, 2, 2 * N], U8, name="kg_codes", align_bytes=64)
         nc.sync.dma_start(kg_codes[:].bitcast(I32), kg_words.bitcast(I32).rearrange("a p w -> p a w"))
         for q in range(4):
             nc.sync.dma_start(
@@ -83,212 +91,169 @@ def tile_list_delayed_residual_correction_kernel(tc, xT, wgt, offs, w1, c, kg_wo
                 kg_scales.bitcast(I32)[:, 4 * q : 4 * q + 4, :].rearrange("a r w -> r a w"),
             )
 
-        def quantize(name, woven, width):
-            codes = keep.tile([P, width], U32, name=name + "_codes", align_bytes=64)
-            scales = keep.tile([P, width], U8, name=name + "_scales", align_bytes=64)
-            nc.vector.quantize_mx(out=codes[:].bitcast(FP8X4), scales=scales[:], in_=woven[:])
+        def mx_tiles(name):
+            codes = keep.tile([P, PASS], U32, name=name + "_codes", align_bytes=64)
+            scales = keep.tile([P, PASS], U8, name=name + "_scales", align_bytes=64)
             return codes, scales
 
-        def copy_on(engine, dst, src):
-            if engine == "scalar":
-                nc.scalar.copy(out=dst, in_=src)
-            elif engine == "gpsimd":
-                nc.gpsimd.tensor_scalar(out=dst, in0=src, scalar1=1.0, scalar2=0.0, op0=MULT, op1=ADD)
-            else:
-                nc.vector.tensor_copy(out=dst, in_=src)
+        def quantize(operand, cols, woven):
+            nc.vector.quantize_mx(out=operand[0][:, cols].bitcast(FP8X4), scales=operand[1][:, cols], in_=woven)
 
-        w_woven, wq, picked, x_woven, xq, hq, h_woven = {}, {}, {}, {}, {}, {}, {}
+        whole = slice(0, PASS)
+        hq = {(b, h): mx_tiles("hq%d%d" % (b, h)) for b in range(2) for h in range(2)}
+        wq, xq, w_woven, x_woven, picked = {}, {}, {}, {}, {}
 
-        early = [keep.tile([P, 2, JC], F32, name="early%d" % h) for h in range(2)]
-        late = keep.tile([P, 2, JC], F32, name="late")
+        last_picked = keep.tile([P, 2 * PACK - HELD, HALF], F32, name="last_picked")
+        picked[1, 0] = last_picked[:, PACK - HELD :, :]
+        picked[1, 1] = last_picked[:, 0:PACK, :]
 
-        for b in range(2):
-            for h in range(2):
-                hq[b, h] = (
-                    keep.tile([P, JC], U32, name="hq%d%d_codes" % (b, h), align_bytes=64),
-                    keep.tile([P, JC], U8, name="hq%d%d_scales" % (b, h), align_bytes=64),
-                )
-
-        def weave_w(a, b, engine):
-            w_woven[a, b] = ring.tile([P, PACK * PASS], BF16, name="w_woven", align_bytes=64)
-            dst = w_woven[a, b][:].rearrange("p (u e m i) -> p u m i e", u=2, e=2, i=PACK)
-            src = w_raw[a, b][:].rearrange("p i (m u e) -> p u m i e", u=2, e=2)
-            for u in range(2):
-                copy_on(engine.split("+")[u % len(engine.split("+"))], dst[:, u], src[:, u])
-
-        def quant_w(a, b):
-            wq[a, b] = quantize("wq%d%d" % (a, b), w_woven[a, b], PASS)
+        spare = keep.tile([P, 2, HALF], F32, name="spare", align_bytes=64)
 
         def gather(a, i, h):
             if a == 0 and i == 0:
-                picked[a, h] = ring.tile([P, PACK, JC], F32, name="picked")
-            cols = slice(h * JC // 16, (h + 1) * JC // 16)
-            dst = picked[a, h][:, i, :] if a == 0 else (early[h], late)[i // 2][:, i % 2, :]
-            nc.vector.tensor_tensor(dst, planes[a, i][:].indirect(offsets[:, cols]), trust[h][:], MULT)
+                picked[a, h] = ring.tile([P, PACK, HALF], F32, name="picked")
+            entries = offsets[:, h * HALF // LIST_ROWS : (h + 1) * HALF // LIST_ROWS]
+            nc.vector.tensor_tensor(picked[a, h][:, i, :], planes[a, i][:].indirect(entries), trust[h][:], MULT)
 
-        def weave_pair(a, h, u, engine):
-            if u == 0:
-                x_woven[a, h] = w_raw[1, 0][:, 2 * h : 2 * h + 2, :].rearrange("p g n -> p (g n)").bitcast(BF16)
-            copy_on(
-                engine,
-                x_woven[a, h][:].rearrange("p (n i) -> p n i", i=PACK)[:, :, 2 * u : 2 * u + 2],
-                (early[h], late)[u][:].rearrange("p i n -> p n i"),
+        def weave_x(a, h, copy, into=None):
+            if into is None:
+                into = ring.tile([P, PACK * HALF], BF16, name="x_woven", align_bytes=64)
+            x_woven[a, h] = into
+            copy(
+                out=x_woven[a, h][:].rearrange("p (m e i) -> p m i e", e=RUN, i=PACK),
+                in_=picked[a, h].rearrange("p i (m e) -> p m i e", e=RUN),
             )
 
-        def weave_x(a, h, engine, held=None):
-            if held is None:
-                x_woven[a, h] = ring.tile([P, PACK * JC], BF16, name="x_woven", align_bytes=64)
-            else:
-                x_woven[a, h] = held[:].rearrange("p g n -> p (g n)").bitcast(BF16)
-            copy_on(
-                engine,
-                x_woven[a, h][:].rearrange("p (m e i) -> p m i e", e=2, i=PACK),
-                picked[a, h].rearrange("p i (m e) -> p m i e", e=2),
+        def quantize_x(a, h):
+            xq[a, h] = mx_tiles("xq%d%d" % (a, h))
+            quantize(xq[a, h], whole, x_woven[a, h][:])
+
+        def weave_w(a, b, copy):
+            w_woven[a, b] = ring.tile([P, PACK * PASS], BF16, name="w_woven", align_bytes=64)
+            copy(
+                out=w_woven[a, b][:].rearrange("p (t m i) -> p m i t", t=PACK, i=PACK),
+                in_=w_raw[a, b][:].rearrange("p i (m t) -> p m i t", t=PACK),
             )
 
-        def quant_x(a, h):
-            xq[a, h] = quantize("xq%d%d" % (a, h), x_woven[a, h], JC)
+        def quantize_w(a, b):
+            wq[a, b] = mx_tiles("wq%d%d" % (a, b))
+            quantize(wq[a, b], whole, w_woven[a, b][:])
 
-        def damp(b, j0, width, order=(1, 0), held=None, on_scalar=(), share=0):
-            h, steps = j0 // JC, slice(j0 % JC, j0 % JC + width)
-            per_bank = JC // width
-            root = ring.tile([P, PACK, width], F32, name="root", bufs=2)
-            part = ring.tile([P, PACK, width], F32, name="part", bufs=2)
-            group = per_bank
-            for t0 in range(0, PACK, group):
-                if held is not None and t0 == held[0]:
-                    square = held[1][:, 0:group, :]
+        def damp(b, j0, width, passes=(1, 0), scalar_heavy=False, lend=None):
+            h, steps = j0 // HALF, slice(j0 % HALF, j0 % HALF + width)
+            slots = PASS // width
+            factor = ring.tile([P, PACK, width], F32, name="factor")
+            scaled = ring.tile([P, PACK, width], F32, name="scaled", align_bytes=64)
+            for t0 in range(0, PACK, slots):
+                if lend is not None and t0 == lend:
+                    square = spare[:, 0:slots, :]
                 else:
-                    square = ring.tile([P, group, width], F32, name="square", bufs=3)
-                sums = {}
-                for tb in range(t0, t0 + group, per_bank):
-                    bank = psum.tile([P, per_bank, width], F32, name="bank")
-                    for t in range(tb, tb + per_bank):
-                        sums[t] = bank[:, t - tb, :]
-                        cols = slice(t * P, (t + 1) * P)
-                        for a in order:
-                            nc.tensor.matmul_mx(
-                                out=sums[t],
-                                lhsT=wq[a, b][0][:, cols].bitcast(FP8X4),
-                                lhsT_scale=wq[a, b][1][:, cols],
-                                rhs=xq[a, h][0][:, steps].bitcast(FP8X4),
-                                rhs_scale=xq[a, h][1][:, steps],
-                                start=(a == order[0]),
-                                stop=(a == order[1]),
-                            )
-                    nc.scalar.activation(out=square[:, tb - t0 : tb - t0 + per_bank, :], in_=bank[:], func=ACT.Square)
-                if t0 in on_scalar:
-                    half = ring.tile([P, group, width], F32, name="half")
-                    nc.scalar.activation(out=half[:], in_=square[:, :, :], func=ACT.Abs_reciprocal_sqrt, bias=1.0)
-                    nc.scalar.activation(out=root[:, t0 : t0 + group, :], in_=half[:], func=ACT.Square)
+                    square = ring.tile([P, slots, width], F32, name="square", bufs=3)
+                bank = psum.tile([P, slots, width], F32, name="bank")
+                for t in range(t0, t0 + slots):
+                    cols = slice(t * P, (t + 1) * P)
+                    for a in passes:
+                        nc.tensor.matmul_mx(
+                            out=bank[:, t - t0, :],
+                            lhsT=wq[a, b][0][:, cols].bitcast(FP8X4),
+                            lhsT_scale=wq[a, b][1][:, cols],
+                            rhs=xq[a, h][0][:, steps].bitcast(FP8X4),
+                            rhs_scale=xq[a, h][1][:, steps],
+                            start=(a == passes[0]),
+                            stop=(a == passes[1]),
+                        )
+                nc.scalar.activation(out=square[:, :, :], in_=bank[:], func=ACT.Square)
+                if scalar_heavy:
+                    root = ring.tile([P, slots, width], F32, name="root", bufs=1)
+                    nc.scalar.activation(out=root[:], in_=square[:, :, :], func=ACT.Abs_reciprocal_sqrt, bias=1.0)
+                    nc.scalar.activation(out=factor[:, t0 : t0 + slots, :], in_=root[:], func=ACT.Square)
                 else:
-                    nc.scalar.activation(out=root[:, t0 : t0 + group, :], in_=square[:, :, :], func=ACT.Abs_reciprocal_sqrt, bias=1.0)
-                for t in range(t0, t0 + group):
-                    if t in on_scalar:
-                        nc.scalar.activation(out=part[:, t, :], in_=sums[t], func=ACT.Copy, scale=gain[:, b, t : t + 1])
+                    nc.scalar.activation(
+                        out=factor[:, t0 : t0 + slots, :], in_=square[:, :, :], func=ACT.Abs_reciprocal_sqrt, bias=1.0
+                    )
+                for t in range(t0, t0 + slots):
+                    res, gain_t = bank[:, t - t0, :], gain[:, b, t : t + 1]
+                    if scalar_heavy:
+                        nc.scalar.activation(out=scaled[:, t, :], in_=res, func=ACT.Copy, scale=gain_t)
                     else:
                         nc.vector.scalar_tensor_tensor(
-                            out=part[:, t, :], in0=sums[t], scalar=gain[:, b, t : t + 1], in1=root[:, t, :], op0=MULT, op1=MULT
+                            out=scaled[:, t, :], in0=res, scalar=gain_t, in1=factor[:, t, :], op0=MULT, op1=MULT
                         )
-            h_woven[b, j0] = ring.tile([P, PACK * width], BF16, name="h_woven", align_bytes=64)
-            lo = max(share - 4, 0)
-            if share < width:
-                nc.vector.tensor_tensor(
-                    h_woven[b, j0][:, PACK * lo :].rearrange("p (m e t) -> p m t e", e=2, t=PACK),
-                    part[:, :, lo:].rearrange("p t (m e) -> p m t e", e=2),
-                    root[:, :, lo:].rearrange("p t (m e) -> p m t e", e=2),
-                    MULT,
-                )
-            if share:
-                nc.gpsimd.tensor_tensor(
-                    h_woven[b, j0][:, 0 : PACK * share].rearrange("p (n t) -> p n t", t=PACK),
-                    part[:, :, 0:share].rearrange("p t n -> p n t"),
-                    root[:, :, 0:share].rearrange("p t n -> p n t"),
-                    MULT,
-                )
-            nc.vector.quantize_mx(out=hq[b, h][0][:, steps].bitcast(FP8X4), scales=hq[b, h][1][:, steps], in_=h_woven[b, j0][:])
+            h_woven = ring.tile([P, PACK * width], BF16, name="h_woven", align_bytes=64)
+            nc.vector.tensor_tensor(
+                h_woven[:].rearrange("p (m e t) -> p m t e", e=RUN, t=PACK),
+                scaled[:].rearrange("p t (m e) -> p m t e", e=RUN),
+                factor[:].rearrange("p t (m e) -> p m t e", e=RUN),
+                MULT,
+            )
+            quantize(hq[b, h], steps, h_woven[:])
 
-        def correct(j0, width, engines, order=(1, 0)):
-            piece = JC if width == JC else P
-            per_bank = JC // width
-            for n0 in range(0, N // P, per_bank):
-                bank = psum.tile([P, per_bank, width], F32, name="bank")
-                for nt in range(n0, n0 + per_bank):
+        staging = [w_raw[a, 0][:, i, :] for a in range(2) for i in range(PACK)]
+
+        def correct(j0, width, first_row):
+            h, s0 = j0 // HALF, j0 % HALF
+            piece = PASS if width == PASS else P
+            tiles = PASS // width
+            for n0 in range(0, N // P, tiles):
+                bank = psum.tile([P, tiles, width], F32, name="bank")
+                for nt in range(n0, n0 + tiles):
                     for c0 in range(0, width, piece):
-                        for b in order:
+                        steps = slice(s0 + c0, s0 + c0 + piece)
+                        for b in (1, 0):
                             nc.tensor.matmul_mx(
                                 out=bank[:, nt - n0, c0 : c0 + piece],
                                 lhsT=kg_codes[:, b, 2 * nt * P : 2 * (nt + 1) * P].bitcast(FP4X4),
                                 lhsT_scale=kg_plane[:, b, nt * P : (nt + 1) * P],
-                                rhs=hq[b, j0 // JC][0][:, j0 % JC + c0 : j0 % JC + c0 + piece].bitcast(FP8X4),
-                                rhs_scale=hq[b, j0 // JC][1][:, j0 % JC + c0 : j0 % JC + c0 + piece],
-                                start=(b == order[0]),
-                                stop=(b == order[1]),
+                                rhs=hq[b, h][0][:, steps].bitcast(FP8X4),
+                                rhs_scale=hq[b, h][1][:, steps],
+                                start=(b == 1),
+                                stop=(b == 0),
                             )
-                result = ring.tile([P, per_bank, width], F32, name="result", bufs=4)
-                copy_on(engines[(n0 // per_bank) % len(engines)], result[:], bank[:])
-                rows = out[n0 * P : (n0 + per_bank) * P, j0 : j0 + width]
-                nc.sync.dma_start(rows.rearrange("(g p) j -> p g j", p=P), result[:])
+                result = staging[first_row + n0 // tiles].rearrange("p (g j) -> p g j", g=tiles)
+                nc.scalar.copy(out=result, in_=bank[:])
+                rows = out[n0 * P : (n0 + tiles) * P, j0 : j0 + width]
+                nc.sync.dma_start(rows.rearrange("(g p) j -> p g j", p=P), result)
+            return first_row + N // P // tiles
 
-        def correct_last(j0, width):
-            h, steps = j0 // JC, slice(j0 % JC, j0 % JC + width)
-            result = ring.tile([P, N // P, width], F32, name="result", bufs=4)
-            for nt in range(N // P):
-                bank = psum.tile([P, width], F32, name="bank")
-                for b in range(2):
-                    nc.tensor.matmul_mx(
-                        out=bank[:],
-                        lhsT=kg_codes[:, b, 2 * nt * P : 2 * (nt + 1) * P].bitcast(FP4X4),
-                        lhsT_scale=kg_plane[:, b, nt * P : (nt + 1) * P],
-                        rhs=hq[b, h][0][:, steps].bitcast(FP8X4),
-                        rhs_scale=hq[b, h][1][:, steps],
-                        start=(b == 0),
-                        stop=(b == 1),
-                    )
-                copy_on(("scalar", "vector")[nt % 2], result[:, nt, :], bank[:])
-            nc.sync.dma_start(out[:, j0 : j0 + width].rearrange("(g p) j -> p g j", p=P), result[:])
+        on_scalar, on_vector = nc.scalar.copy, nc.vector.tensor_copy
 
-        gather(0, 0, 0)
-        gather(0, 0, 1)
-        gather(0, 1, 0)
-        gather(0, 1, 1)
-        gather(0, 2, 0)
-        gather(0, 2, 1)
-        gather(0, 3, 0)
-        gather(0, 3, 1)
-        weave_x(0, 0, "scalar")
-        weave_x(0, 1, "scalar")
-        gather(1, 0, 0)
-        gather(1, 0, 1)
-        quant_x(0, 0)
-        weave_w(0, 0, "scalar")
-        gather(1, 1, 0)
-        gather(1, 1, 1)
-        quant_x(0, 1)
-        weave_w(1, 0, "scalar")
-        quant_w(0, 0)
-        weave_pair(1, 0, 0, "scalar")
-        weave_pair(1, 1, 0, "scalar")
-        gather(1, 2, 0)
-        quant_w(1, 0)
-        gather(1, 3, 0)
-        weave_pair(1, 0, 1, "vector")
-        quant_x(1, 0)
-        weave_w(0, 1, "scalar")
-        gather(1, 2, 1)
-        gather(1, 3, 1)
-        weave_w(1, 1, "vector")
-        quant_w(0, 1)
-        quant_w(1, 1)
-        damp(0, 0, 512, (0, 1))
-        weave_pair(1, 1, 1, "scalar")
-        quant_x(1, 1)
-        damp(1, 0, 512, on_scalar=(3,))
-        damp(0, 512, 512, on_scalar=(3,))
-        damp(1, 512, 256, on_scalar=())
-        damp(1, 768, 128, on_scalar=())
-        damp(1, 896, 128)
-        correct(0, 512, ["scalar"])
-        correct(512, 256, ["scalar"])
-        correct(768, 128, ["scalar"])
-        correct_last(896, 128)
+        for i in range(PACK):
+            for h in range(2):
+                gather(0, i, h)
+        for h in range(2):
+            weave_x(0, h, on_scalar)
+        for h in range(2):
+            gather(1, 0, h)
+        quantize_x(0, 0)
+        weave_w(0, 0, on_scalar)
+        for h in range(2):
+            gather(1, 1, h)
+        quantize_x(0, 1)
+        quantize_w(0, 0)
+        for i in range(2, PACK):
+            for h in range(2 if i < PACK - HELD else 1):
+                gather(1, i, h)
+
+        weave_x(1, 0, on_scalar)
+        weave_w(1, 0, on_vector)
+        quantize_w(1, 0)
+        quantize_x(1, 0)
+
+        weave_w(0, 1, on_scalar)
+        for i in range(PACK - HELD, PACK):
+            gather(1, i, 1)
+        weave_w(1, 1, on_vector)
+        quantize_w(0, 1)
+        quantize_w(1, 1)
+
+        damp(0, 0, HALF, passes=(0, 1), lend=2)
+        weave_x(1, 1, on_scalar, spare[:].rearrange("p g n -> p (g n)").bitcast(BF16))
+        quantize_x(1, 1)
+        damp(1, 0, HALF)
+        damp(0, HALF, HALF)
+        starts = [HALF + sum(TAIL[:n]) for n in range(len(TAIL))]
+        for j0, width in zip(starts, TAIL):
+            damp(1, j0, width, scalar_heavy=(width == max(TAIL)))
+        row = correct(0, HALF, 0)
+        for j0, width in zip(starts, TAIL):
+            row = correct(j0, width, row)

@@ -24,15 +24,25 @@ LIST_ROWS = 16
 RUN = 4
 QUARTER = S // 4
 BLOCK = 32
-HELD = 2
+OPENING = (256, 256)
 TAIL = (256, 128, 128)
+
+
+def spans(first, widths):
+    return [(first + sum(widths[:n]), widths[n]) for n in range(len(widths))]
+
+
+def pass_order(parts, early):
+    if early:
+        order = [(a, part) for a in range(2) for part in parts]
+        return [(a, part, n == 0, n == len(order) - 1) for n, (a, part) in enumerate(order)]
+    return [(a, part, a == 1, a == 0) for part in parts for a in (1, 0)]
 
 
 def tile_list_delayed_residual_correction_kernel(tc, xT, wgt, offs, w1, c, kg_words, kg_scales, out):
     nc = tc.nc
     with ExitStack() as ctx:
         keep = ctx.enter_context(tc.tile_pool(name="keep", bufs=1))
-        ring = ctx.enter_context(tc.tile_pool(name="ring", bufs=2))
         psum = ctx.enter_context(tc.psum_pool(name="psum", bufs=8))
 
         offsets = keep.tile([P, S // LIST_ROWS], U16, name="offsets")
@@ -51,16 +61,19 @@ def tile_list_delayed_residual_correction_kernel(tc, xT, wgt, offs, w1, c, kg_wo
         nc.sync.dma_start(offsets[:], offs)
         trust_turned = keep.tile([P, QUARTER], F32, name="trust_turned", align_bytes=64)
         nc.vector.transpose(trust_turned[:], trust_part[:])
-        trust_spread = ring.tile([P, S], F32, name="scaled", align_bytes=64)
+        factor = keep.tile([P, PACK * S], F32, name="factor", align_bytes=64)
+        scaled = keep.tile([P, PACK * S], F32, name="scaled", align_bytes=64)
+        h_woven = keep.tile([P, PACK * S], BF16, name="h_woven", align_bytes=64)
+        trust_spread = scaled[:, 0:S]
         by_row = trust_turned[:].rearrange("p (c r q) -> p q c r", r=BLOCK // 4, q=4)
         for h in range(2):
             nc.vector.tensor_copy(
                 out=trust_spread[:, h * HALF : (h + 1) * HALF].rearrange("p (q c r e) -> p q c r e", q=2, r=BLOCK // 4, e=4),
                 in_=by_row[:, 2 * h : 2 * h + 2].unsqueeze(4).to_broadcast([P, 2, QUARTER // BLOCK, BLOCK // 4, 4]),
             )
-        trust = [keep.tile([P, HALF], F32, name="trust%d" % h, align_bytes=64) for h in range(2)]
+        trust = keep.tile([P, S], F32, name="trust", align_bytes=64)
         for h in range(2):
-            nc.vector.transpose(trust[h][:], trust_spread[:, h * HALF : (h + 1) * HALF])
+            nc.vector.transpose(trust[:, h * HALF : (h + 1) * HALF], trust_spread[:, h * HALF : (h + 1) * HALF])
 
         x_rows = xT.rearrange("(a p i) t -> a i p t", a=2, i=PACK)
         w_rows = w1.rearrange("(a p i) (b r) -> a b p i r", a=2, i=PACK, b=2)
@@ -77,8 +90,8 @@ def tile_list_delayed_residual_correction_kernel(tc, xT, wgt, offs, w1, c, kg_wo
         for n in range(2 * PACK - 1):
             load_plane(n // PACK, n % PACK)
         load_w(0, 0)
-        load_plane(1, PACK - 1)
         load_w(1, 0)
+        load_plane(1, PACK - 1)
         load_w(0, 1)
         load_w(1, 1)
         gain = keep.tile([P, 2, PACK], F32, name="gain")
@@ -91,169 +104,145 @@ def tile_list_delayed_residual_correction_kernel(tc, xT, wgt, offs, w1, c, kg_wo
                 kg_scales.bitcast(I32)[:, 4 * q : 4 * q + 4, :].rearrange("a r w -> r a w"),
             )
 
-        def mx_tiles(name):
-            codes = keep.tile([P, PASS], U32, name=name + "_codes", align_bytes=64)
-            scales = keep.tile([P, PASS], U8, name=name + "_scales", align_bytes=64)
+        def mx_tiles(name, width):
+            codes = keep.tile([P, width], U32, name=name + "_codes", align_bytes=64)
+            scales = keep.tile([P, width], U8, name=name + "_scales", align_bytes=64)
             return codes, scales
 
         def quantize(operand, cols, woven):
             nc.vector.quantize_mx(out=operand[0][:, cols].bitcast(FP8X4), scales=operand[1][:, cols], in_=woven)
 
-        whole = slice(0, PASS)
-        hq = {(b, h): mx_tiles("hq%d%d" % (b, h)) for b in range(2) for h in range(2)}
-        wq, xq, w_woven, x_woven, picked = {}, {}, {}, {}, {}
+        def stretch(tile, at, width):
+            return tile[:, PACK * at : PACK * (at + width)]
 
-        last_picked = keep.tile([P, 2 * PACK - HELD, HALF], F32, name="last_picked")
-        picked[1, 0] = last_picked[:, PACK - HELD :, :]
-        picked[1, 1] = last_picked[:, 0:PACK, :]
+        xq = [mx_tiles("xq%d" % a, S) for a in range(2)]
+        hq = [mx_tiles("hq%d" % b, S) for b in range(2)]
+        wq = {}
+        picked = [keep.tile([P, PACK * S], F32, name="picked%d" % a) for a in range(2)]
+        x_woven = keep.tile([P, PACK * S], BF16, name="x_woven", align_bytes=64)
+        w_woven = [h_woven, keep.tile([P, 2 * PACK * PASS], BF16, name="w_woven", align_bytes=64)]
 
-        spare = keep.tile([P, 2, HALF], F32, name="spare", align_bytes=64)
+        def gather(a, i, j0, width):
+            entries = offsets[:, j0 // LIST_ROWS : (j0 + width) // LIST_ROWS]
+            row = stretch(picked[a], j0, width)[:, i * width : (i + 1) * width]
+            nc.vector.tensor_tensor(row, planes[a, i][:].indirect(entries), trust[:, j0 : j0 + width], MULT)
 
-        def gather(a, i, h):
-            if a == 0 and i == 0:
-                picked[a, h] = ring.tile([P, PACK, HALF], F32, name="picked")
-            entries = offsets[:, h * HALF // LIST_ROWS : (h + 1) * HALF // LIST_ROWS]
-            nc.vector.tensor_tensor(picked[a, h][:, i, :], planes[a, i][:].indirect(entries), trust[h][:], MULT)
-
-        def weave_x(a, h, copy, into=None):
-            if into is None:
-                into = ring.tile([P, PACK * HALF], BF16, name="x_woven", align_bytes=64)
-            x_woven[a, h] = into
-            copy(
-                out=x_woven[a, h][:].rearrange("p (m e i) -> p m i e", e=RUN, i=PACK),
-                in_=picked[a, h].rearrange("p i (m e) -> p m i e", e=RUN),
+        def prepare_x(a, j0, width):
+            woven = stretch(x_woven, j0, width)
+            nc.scalar.copy(
+                out=woven.rearrange("p (m e i) -> p m i e", e=RUN, i=PACK),
+                in_=stretch(picked[a], j0, width).rearrange("p (i m e) -> p m i e", e=RUN, i=PACK),
             )
+            quantize(xq[a], slice(j0, j0 + width), woven)
 
-        def quantize_x(a, h):
-            xq[a, h] = mx_tiles("xq%d%d" % (a, h))
-            quantize(xq[a, h], whole, x_woven[a, h][:])
-
-        def weave_w(a, b, copy):
-            w_woven[a, b] = ring.tile([P, PACK * PASS], BF16, name="w_woven", align_bytes=64)
+        def prepare_w(a, b, copy):
+            woven = stretch(w_woven[b], a * PASS, PASS)
             copy(
-                out=w_woven[a, b][:].rearrange("p (t m i) -> p m i t", t=PACK, i=PACK),
+                out=woven.rearrange("p (t m i) -> p m i t", t=PACK, i=PACK),
                 in_=w_raw[a, b][:].rearrange("p i (m t) -> p m i t", t=PACK),
             )
+            wq[a, b] = mx_tiles("wq%d%d" % (a, b), PASS)
+            quantize(wq[a, b], slice(0, PASS), woven)
 
-        def quantize_w(a, b):
-            wq[a, b] = mx_tiles("wq%d%d" % (a, b))
-            quantize(wq[a, b], whole, w_woven[a, b][:])
-
-        def damp(b, j0, width, passes=(1, 0), scalar_heavy=False, lend=None):
-            h, steps = j0 // HALF, slice(j0 % HALF, j0 % HALF + width)
+        def damp(b, j0, width, early=False, scalar_heavy=False):
+            steps = slice(j0, j0 + width)
+            at = b * HALF + j0 % HALF
+            left = stretch(scaled, at, width).rearrange("p (t j) -> p t j", t=PACK)
+            right = stretch(factor, at, width).rearrange("p (t j) -> p t j", t=PACK)
             slots = PASS // width
-            factor = ring.tile([P, PACK, width], F32, name="factor")
-            scaled = ring.tile([P, PACK, width], F32, name="scaled", align_bytes=64)
             for t0 in range(0, PACK, slots):
-                if lend is not None and t0 == lend:
-                    square = spare[:, 0:slots, :]
-                else:
-                    square = ring.tile([P, slots, width], F32, name="square", bufs=3)
+                rows = slice(t0, t0 + slots)
                 bank = psum.tile([P, slots, width], F32, name="bank")
-                for t in range(t0, t0 + slots):
+                for a, t, start, stop in pass_order(range(t0, t0 + slots), early):
                     cols = slice(t * P, (t + 1) * P)
-                    for a in passes:
-                        nc.tensor.matmul_mx(
-                            out=bank[:, t - t0, :],
-                            lhsT=wq[a, b][0][:, cols].bitcast(FP8X4),
-                            lhsT_scale=wq[a, b][1][:, cols],
-                            rhs=xq[a, h][0][:, steps].bitcast(FP8X4),
-                            rhs_scale=xq[a, h][1][:, steps],
-                            start=(a == passes[0]),
-                            stop=(a == passes[1]),
-                        )
-                nc.scalar.activation(out=square[:, :, :], in_=bank[:], func=ACT.Square)
-                if scalar_heavy:
-                    root = ring.tile([P, slots, width], F32, name="root", bufs=1)
-                    nc.scalar.activation(out=root[:], in_=square[:, :, :], func=ACT.Abs_reciprocal_sqrt, bias=1.0)
-                    nc.scalar.activation(out=factor[:, t0 : t0 + slots, :], in_=root[:], func=ACT.Square)
-                else:
-                    nc.scalar.activation(
-                        out=factor[:, t0 : t0 + slots, :], in_=square[:, :, :], func=ACT.Abs_reciprocal_sqrt, bias=1.0
+                    nc.tensor.matmul_mx(
+                        out=bank[:, t - t0, :],
+                        lhsT=wq[a, b][0][:, cols].bitcast(FP8X4),
+                        lhsT_scale=wq[a, b][1][:, cols],
+                        rhs=xq[a][0][:, steps].bitcast(FP8X4),
+                        rhs_scale=xq[a][1][:, steps],
+                        start=start,
+                        stop=stop,
                     )
+                if scalar_heavy:
+                    nc.scalar.activation(out=right[:, rows, :], in_=bank[:], func=ACT.Square)
+                    nc.scalar.activation(out=left[:, rows, :], in_=right[:, rows, :], func=ACT.Abs_reciprocal_sqrt, bias=1.0)
+                    nc.scalar.activation(out=right[:, rows, :], in_=left[:, rows, :], func=ACT.Square)
+                else:
+                    nc.scalar.activation(out=left[:, rows, :], in_=bank[:], func=ACT.Square)
+                    nc.scalar.activation(out=right[:, rows, :], in_=left[:, rows, :], func=ACT.Abs_reciprocal_sqrt, bias=1.0)
                 for t in range(t0, t0 + slots):
                     res, gain_t = bank[:, t - t0, :], gain[:, b, t : t + 1]
                     if scalar_heavy:
-                        nc.scalar.activation(out=scaled[:, t, :], in_=res, func=ACT.Copy, scale=gain_t)
+                        nc.scalar.activation(out=left[:, t, :], in_=res, func=ACT.Copy, scale=gain_t)
                     else:
                         nc.vector.scalar_tensor_tensor(
-                            out=scaled[:, t, :], in0=res, scalar=gain_t, in1=factor[:, t, :], op0=MULT, op1=MULT
+                            out=left[:, t, :], in0=res, scalar=gain_t, in1=right[:, t, :], op0=MULT, op1=MULT
                         )
-            h_woven = ring.tile([P, PACK * width], BF16, name="h_woven", align_bytes=64)
+            woven = stretch(h_woven, at, width)
             nc.vector.tensor_tensor(
-                h_woven[:].rearrange("p (m e t) -> p m t e", e=RUN, t=PACK),
-                scaled[:].rearrange("p t (m e) -> p m t e", e=RUN),
-                factor[:].rearrange("p t (m e) -> p m t e", e=RUN),
+                woven.rearrange("p (m e t) -> p m t e", e=RUN, t=PACK),
+                left.rearrange("p t (m e) -> p m t e", e=RUN),
+                right.rearrange("p t (m e) -> p m t e", e=RUN),
                 MULT,
             )
-            quantize(hq[b, h], steps, h_woven[:])
+            quantize(hq[b], steps, woven)
 
         staging = [w_raw[a, 0][:, i, :] for a in range(2) for i in range(PACK)]
 
-        def correct(j0, width, first_row):
-            h, s0 = j0 // HALF, j0 % HALF
+        def correct(j0, width, copy, early=False):
             piece = PASS if width == PASS else P
             tiles = PASS // width
             for n0 in range(0, N // P, tiles):
                 bank = psum.tile([P, tiles, width], F32, name="bank")
-                for nt in range(n0, n0 + tiles):
-                    for c0 in range(0, width, piece):
-                        steps = slice(s0 + c0, s0 + c0 + piece)
-                        for b in (1, 0):
-                            nc.tensor.matmul_mx(
-                                out=bank[:, nt - n0, c0 : c0 + piece],
-                                lhsT=kg_codes[:, b, 2 * nt * P : 2 * (nt + 1) * P].bitcast(FP4X4),
-                                lhsT_scale=kg_plane[:, b, nt * P : (nt + 1) * P],
-                                rhs=hq[b, h][0][:, steps].bitcast(FP8X4),
-                                rhs_scale=hq[b, h][1][:, steps],
-                                start=(b == 1),
-                                stop=(b == 0),
-                            )
-                result = staging[first_row + n0 // tiles].rearrange("p (g j) -> p g j", g=tiles)
-                nc.scalar.copy(out=result, in_=bank[:])
+                parts = [(nt, c0) for nt in range(n0, n0 + tiles) for c0 in range(0, width, piece)]
+                for b, (nt, c0), start, stop in pass_order(parts, early):
+                    steps = slice(j0 + c0, j0 + c0 + piece)
+                    nc.tensor.matmul_mx(
+                        out=bank[:, nt - n0, c0 : c0 + piece],
+                        lhsT=kg_codes[:, b, 2 * nt * P : 2 * (nt + 1) * P].bitcast(FP4X4),
+                        lhsT_scale=kg_plane[:, b, nt * P : (nt + 1) * P],
+                        rhs=hq[b][0][:, steps].bitcast(FP8X4),
+                        rhs_scale=hq[b][1][:, steps],
+                        start=start,
+                        stop=stop,
+                    )
+                result = staging[j0 // P + n0 // tiles].rearrange("p (g j) -> p g j", g=tiles)
+                copy(out=result, in_=bank[:])
                 rows = out[n0 * P : (n0 + tiles) * P, j0 : j0 + width]
                 nc.sync.dma_start(rows.rearrange("(g p) j -> p g j", p=P), result)
-            return first_row + N // P // tiles
 
         on_scalar, on_vector = nc.scalar.copy, nc.vector.tensor_copy
 
+        halves = spans(0, (HALF, HALF))
+        opening = spans(0, OPENING)
+        tail = spans(HALF, TAIL)
+        last_pass = opening + halves[1:]
+
         for i in range(PACK):
-            for h in range(2):
-                gather(0, i, h)
-        for h in range(2):
-            weave_x(0, h, on_scalar)
-        for h in range(2):
-            gather(1, 0, h)
-        quantize_x(0, 0)
-        weave_w(0, 0, on_scalar)
-        for h in range(2):
-            gather(1, 1, h)
-        quantize_x(0, 1)
-        quantize_w(0, 0)
-        for i in range(2, PACK):
-            for h in range(2 if i < PACK - HELD else 1):
-                gather(1, i, h)
+            for j0, width in halves:
+                gather(0, i, j0, width)
+        for j0, width in halves:
+            prepare_x(0, j0, width)
+        prepare_w(0, 0, on_scalar)
+        for i in range(PACK - 1):
+            for j0, width in last_pass:
+                gather(1, i, j0, width)
+        prepare_w(1, 0, on_scalar)
+        for j0, width in last_pass:
+            gather(1, PACK - 1, j0, width)
+            prepare_x(1, j0, width)
 
-        weave_x(1, 0, on_scalar)
-        weave_w(1, 0, on_vector)
-        quantize_w(1, 0)
-        quantize_x(1, 0)
-
-        weave_w(0, 1, on_scalar)
-        for i in range(PACK - HELD, PACK):
-            gather(1, i, 1)
-        weave_w(1, 1, on_vector)
-        quantize_w(0, 1)
-        quantize_w(1, 1)
-
-        damp(0, 0, HALF, passes=(0, 1), lend=2)
-        weave_x(1, 1, on_scalar, spare[:].rearrange("p g n -> p (g n)").bitcast(BF16))
-        quantize_x(1, 1)
+        for j0, width in opening:
+            damp(0, j0, width, early=True)
+        for a in range(2):
+            prepare_w(a, 1, on_vector)
         damp(1, 0, HALF)
+
         damp(0, HALF, HALF)
-        starts = [HALF + sum(TAIL[:n]) for n in range(len(TAIL))]
-        for j0, width in zip(starts, TAIL):
-            damp(1, j0, width, scalar_heavy=(width == max(TAIL)))
-        row = correct(0, HALF, 0)
-        for j0, width in zip(starts, TAIL):
-            row = correct(j0, width, row)
+        for j0, width in tail:
+            damp(1, j0, width, scalar_heavy=(j0 + width == S))
+
+        correct(0, HALF, on_scalar)
+        for j0, width in tail:
+            correct(j0, width, on_vector if j0 + width == S else on_scalar, early=True)

from contextlib import ExitStack

import concourse.mybir as mybir

K, T, S, R, N = 1024, 2048, 1024, 1024, 512
FLOPS = 2 * K * R * S + 2 * R * N * S

F32 = mybir.dt.float32
BF16 = mybir.dt.bfloat16
I32 = mybir.dt.int32
U32 = mybir.dt.uint32
U16 = mybir.dt.uint16
U8 = mybir.dt.uint8
FP8X4 = mybir.dt.float8_e4m3fn_x4
FP4X4 = mybir.dt.float4_e2m1fn_x4
MULT = mybir.AluOpType.mult
ACT = mybir.ActivationFunctionType

P = 128
PACK = 4
PASS = P * PACK
HALF = S // 2
LIST_ROWS = 16
RUN = 4
QUARTER = S // 4
BLOCK = 32
OPENING = (256, 256)
TAIL = (256, 128, 128)


def spans(first, widths):
    return [(first + sum(widths[:n]), widths[n]) for n in range(len(widths))]


def pass_order(parts, early):
    if early:
        order = [(a, part) for a in range(2) for part in parts]
        return [(a, part, n == 0, n == len(order) - 1) for n, (a, part) in enumerate(order)]
    return [(a, part, a == 1, a == 0) for part in parts for a in (1, 0)]


def tile_list_delayed_residual_correction_kernel(tc, xT, wgt, offs, w1, c, kg_words, kg_scales, out):
    nc = tc.nc
    with ExitStack() as ctx:
        keep = ctx.enter_context(tc.tile_pool(name="keep", bufs=1))
        psum = ctx.enter_context(tc.psum_pool(name="psum", bufs=8))

        offsets = keep.tile([P, S // LIST_ROWS], U16, name="offsets")

        warm_in = keep.tile([P, 8], F32, name="warm_in")
        warm_out = keep.tile([P, 8], F32, name="warm_out")
        nc.vector.memset(warm_in[:], 1.0)
        nc.scalar.activation(out=warm_out[:], in_=warm_in[:], func=ACT.Abs_reciprocal_sqrt, bias=1.0)

        kg_plane = keep.tile([P, 2, N], U8, name="kg_plane", align_bytes=64)
        nc.vector.memset(kg_plane[:].rearrange("p a n -> p (a n)").bitcast(I32), 0)

        trust_part = keep.tile([P, QUARTER], F32, name="trust_part", align_bytes=64)
        for q in range(4):
            nc.sync.dma_start(trust_part[q:P:4, :], wgt[q:P:4, q * QUARTER : (q + 1) * QUARTER])
        nc.sync.dma_start(offsets[:], offs)
        trust_turned = keep.tile([P, QUARTER], F32, name="trust_turned", align_bytes=64)
        nc.vector.transpose(trust_turned[:], trust_part[:])
        factor = keep.tile([P, PACK * S], F32, name="factor", align_bytes=64)
        scaled = keep.tile([P, PACK * S], F32, name="scaled", align_bytes=64)
        h_woven = keep.tile([P, PACK * S], BF16, name="h_woven", align_bytes=64)
        trust_spread = scaled[:, 0:S]
        by_row = trust_turned[:].rearrange("p (c r q) -> p q c r", r=BLOCK // 4, q=4)
        for h in range(2):
            nc.vector.tensor_copy(
                out=trust_spread[:, h * HALF : (h + 1) * HALF].rearrange("p (q c r e) -> p q c r e", q=2, r=BLOCK // 4, e=4),
                in_=by_row[:, 2 * h : 2 * h + 2].unsqueeze(4).to_broadcast([P, 2, QUARTER // BLOCK, BLOCK // 4, 4]),
            )
        trust = keep.tile([P, S], F32, name="trust", align_bytes=64)
        for h in range(2):
            nc.vector.transpose(trust[:, h * HALF : (h + 1) * HALF], trust_spread[:, h * HALF : (h + 1) * HALF])

        x_rows = xT.rearrange("(a p i) t -> a i p t", a=2, i=PACK)
        w_rows = w1.rearrange("(a p i) (b r) -> a b p i r", a=2, i=PACK, b=2)
        planes, w_raw = {}, {}

        def load_plane(a, i):
            planes[a, i] = keep.tile([P, T], F32, name="plane%d%d" % (a, i))
            nc.sync.dma_start(planes[a, i][:], x_rows[a, i])

        def load_w(a, b):
            w_raw[a, b] = keep.tile([P, PACK, PASS], F32, name="w_raw%d%d" % (a, b))
            nc.sync.dma_start(w_raw[a, b][:], w_rows[a, b])

        for n in range(2 * PACK - 1):
            load_plane(n // PACK, n % PACK)
        load_w(0, 0)
        load_w(1, 0)
        load_plane(1, PACK - 1)
        load_w(0, 1)
        load_w(1, 1)
        gain = keep.tile([P, 2, PACK], F32, name="gain")
        nc.sync.dma_start(gain[:], c.rearrange("(b p t) -> p b t", b=2, t=PACK))
        kg_codes = keep.tile([P, 2, 2 * N], U8, name="kg_codes", align_bytes=64)
        nc.sync.dma_start(kg_codes[:].bitcast(I32), kg_words.bitcast(I32).rearrange("a p w -> p a w"))
        for q in range(4):
            nc.sync.dma_start(
                kg_plane[32 * q : 32 * q + 4, :, :].bitcast(I32),
                kg_scales.bitcast(I32)[:, 4 * q : 4 * q + 4, :].rearrange("a r w -> r a w"),
            )

        def mx_tiles(name, width):
            codes = keep.tile([P, width], U32, name=name + "_codes", align_bytes=64)
            scales = keep.tile([P, width], U8, name=name + "_scales", align_bytes=64)
            return codes, scales

        def quantize(operand, cols, woven):
            nc.vector.quantize_mx(out=operand[0][:, cols].bitcast(FP8X4), scales=operand[1][:, cols], in_=woven)

        def stretch(tile, at, width):
            return tile[:, PACK * at : PACK * (at + width)]

        xq = [mx_tiles("xq%d" % a, S) for a in range(2)]
        hq = [mx_tiles("hq%d" % b, S) for b in range(2)]
        wq = {}
        picked = [keep.tile([P, PACK * S], F32, name="picked%d" % a) for a in range(2)]
        x_woven = keep.tile([P, PACK * S], BF16, name="x_woven", align_bytes=64)
        w_woven = [h_woven, keep.tile([P, 2 * PACK * PASS], BF16, name="w_woven", align_bytes=64)]

        def gather(a, i, j0, width):
            entries = offsets[:, j0 // LIST_ROWS : (j0 + width) // LIST_ROWS]
            row = stretch(picked[a], j0, width)[:, i * width : (i + 1) * width]
            nc.vector.tensor_tensor(row, planes[a, i][:].indirect(entries), trust[:, j0 : j0 + width], MULT)

        def prepare_x(a, j0, width):
            woven = stretch(x_woven, j0, width)
            nc.scalar.copy(
                out=woven.rearrange("p (m e i) -> p m i e", e=RUN, i=PACK),
                in_=stretch(picked[a], j0, width).rearrange("p (i m e) -> p m i e", e=RUN, i=PACK),
            )
            quantize(xq[a], slice(j0, j0 + width), woven)

        def prepare_w(a, b, copy):
            woven = stretch(w_woven[b], a * PASS, PASS)
            copy(
                out=woven.rearrange("p (t m i) -> p m i t", t=PACK, i=PACK),
                in_=w_raw[a, b][:].rearrange("p i (m t) -> p m i t", t=PACK),
            )
            wq[a, b] = mx_tiles("wq%d%d" % (a, b), PASS)
            quantize(wq[a, b], slice(0, PASS), woven)

        def damp(b, j0, width, early=False, scalar_heavy=False):
            steps = slice(j0, j0 + width)
            at = b * HALF + j0 % HALF
            left = stretch(scaled, at, width).rearrange("p (t j) -> p t j", t=PACK)
            right = stretch(factor, at, width).rearrange("p (t j) -> p t j", t=PACK)
            slots = PASS // width
            for t0 in range(0, PACK, slots):
                rows = slice(t0, t0 + slots)
                bank = psum.tile([P, slots, width], F32, name="bank")
                for a, t, start, stop in pass_order(range(t0, t0 + slots), early):
                    cols = slice(t * P, (t + 1) * P)
                    nc.tensor.matmul_mx(
                        out=bank[:, t - t0, :],
                        lhsT=wq[a, b][0][:, cols].bitcast(FP8X4),
                        lhsT_scale=wq[a, b][1][:, cols],
                        rhs=xq[a][0][:, steps].bitcast(FP8X4),
                        rhs_scale=xq[a][1][:, steps],
                        start=start,
                        stop=stop,
                    )
                if scalar_heavy:
                    nc.scalar.activation(out=right[:, rows, :], in_=bank[:], func=ACT.Square)
                    nc.scalar.activation(out=left[:, rows, :], in_=right[:, rows, :], func=ACT.Abs_reciprocal_sqrt, bias=1.0)
                    nc.scalar.activation(out=right[:, rows, :], in_=left[:, rows, :], func=ACT.Square)
                else:
                    nc.scalar.activation(out=left[:, rows, :], in_=bank[:], func=ACT.Square)
                    nc.scalar.activation(out=right[:, rows, :], in_=left[:, rows, :], func=ACT.Abs_reciprocal_sqrt, bias=1.0)
                for t in range(t0, t0 + slots):
                    res, gain_t = bank[:, t - t0, :], gain[:, b, t : t + 1]
                    if scalar_heavy:
                        nc.scalar.activation(out=left[:, t, :], in_=res, func=ACT.Copy, scale=gain_t)
                    else:
                        nc.vector.scalar_tensor_tensor(
                            out=left[:, t, :], in0=res, scalar=gain_t, in1=right[:, t, :], op0=MULT, op1=MULT
                        )
            woven = stretch(h_woven, at, width)
            nc.vector.tensor_tensor(
                woven.rearrange("p (m e t) -> p m t e", e=RUN, t=PACK),
                left.rearrange("p t (m e) -> p m t e", e=RUN),
                right.rearrange("p t (m e) -> p m t e", e=RUN),
                MULT,
            )
            quantize(hq[b], steps, woven)

        staging = [w_raw[a, 0][:, i, :] for a in range(2) for i in range(PACK)]

        def correct(j0, width, copy, early=False):
            piece = PASS if width == PASS else P
            tiles = PASS // width
            for n0 in range(0, N // P, tiles):
                bank = psum.tile([P, tiles, width], F32, name="bank")
                parts = [(nt, c0) for nt in range(n0, n0 + tiles) for c0 in range(0, width, piece)]
                for b, (nt, c0), start, stop in pass_order(parts, early):
                    steps = slice(j0 + c0, j0 + c0 + piece)
                    nc.tensor.matmul_mx(
                        out=bank[:, nt - n0, c0 : c0 + piece],
                        lhsT=kg_codes[:, b, 2 * nt * P : 2 * (nt + 1) * P].bitcast(FP4X4),
                        lhsT_scale=kg_plane[:, b, nt * P : (nt + 1) * P],
                        rhs=hq[b][0][:, steps].bitcast(FP8X4),
                        rhs_scale=hq[b][1][:, steps],
                        start=start,
                        stop=stop,
                    )
                result = staging[j0 // P + n0 // tiles].rearrange("p (g j) -> p g j", g=tiles)
                copy(out=result, in_=bank[:])
                rows = out[n0 * P : (n0 + tiles) * P, j0 : j0 + width]
                nc.sync.dma_start(rows.rearrange("(g p) j -> p g j", p=P), result)

        on_scalar, on_vector = nc.scalar.copy, nc.vector.tensor_copy

        halves = spans(0, (HALF, HALF))
        opening = spans(0, OPENING)
        tail = spans(HALF, TAIL)
        last_pass = opening + halves[1:]

        for i in range(PACK):
            for j0, width in halves:
                gather(0, i, j0, width)
        for j0, width in halves:
            prepare_x(0, j0, width)
        prepare_w(0, 0, on_scalar)
        for i in range(PACK - 1):
            for j0, width in last_pass:
                gather(1, i, j0, width)
        prepare_w(1, 0, on_scalar)
        for j0, width in last_pass:
            gather(1, PACK - 1, j0, width)
            prepare_x(1, j0, width)

        for j0, width in opening:
            damp(0, j0, width, early=True)
        for a in range(2):
            prepare_w(a, 1, on_vector)
        damp(1, 0, HALF)

        damp(0, HALF, HALF)
        for j0, width in tail:
            damp(1, j0, width, scalar_heavy=(j0 + width == S))

        correct(0, HALF, on_scalar)
        for j0, width in tail:
            correct(j0, width, on_vector if j0 + width == S else on_scalar, early=True)
